import numpy as np
import ml_dtypes


def mxq(x, axis, fmt="e4m3"):
    dtype, down = {"e4m3": (ml_dtypes.float8_e4m3fn, 7), "e5m2": (ml_dtypes.float8_e5m2, 14)}[fmt]
    v = np.moveaxis(np.asarray(x, np.float32).astype(ml_dtypes.bfloat16).astype(np.float64), axis, -1)
    blocks = v.reshape(v.shape[:-1] + (-1, 32))
    amax = np.abs(blocks).max(-1, keepdims=True)
    byte = np.maximum(np.where(amax > 0, np.frexp(amax)[1] - 1 + 127, 0) - down, 1)
    scale = np.exp2(byte - 127.0)
    codes = (blocks / scale).astype(np.float32).astype(dtype).astype(np.float64)
    return np.moveaxis((codes * scale).reshape(v.shape), -1, axis)


WIDE = False


def mx_kscale(k):
    if not WIDE:
        return np.ones(k)
    levels = np.array([10, -10, 5, -5, 0])
    if k % 512:
        return np.exp2(np.random.permutation(np.resize(levels, k // 32))).repeat(32)
    a = np.empty((k // 512, 16))
    for p in range(k // 512):
        a[p, :8] = np.random.permutation(np.resize(levels, 8))
        for g in range(8):
            far = levels[np.abs(levels - a[p, g]) >= 10]
            a[p, g + 8] = far[np.random.randint(len(far))]
    return np.exp2(a.ravel()).repeat(32)


def f64(x):
    return np.asarray(x).astype(np.float64)


def striped(idx):
    return np.tile(idx.reshape(-1, 16).T, (8, 1)).astype(np.uint16)


def unstriped(offs):
    return offs[:16].T.reshape(-1).astype(np.int64)


E2M1 = np.array([0.0, 0.5, 1.0, 1.5, 2.0, 3.0, 4.0, 6.0, -0.0, -0.5, -1.0, -1.5, -2.0, -3.0, -4.0, -6.0])


def pack_weight(w, fmt):
    k, n = w.shape
    w = f64(np.asarray(w, np.float32).astype(ml_dtypes.bfloat16)).reshape(k // 32, 32, n)
    amax = np.abs(w).max(1)
    if fmt == "e4m3":
        byte = np.frexp(amax)[1] - 1 + 127 - 7
    else:
        mant, ex = np.frexp(amax / 6.0)
        byte = np.where(mant > 0.5, ex, ex - 1) + 127
    byte = np.clip(np.where(amax > 0, byte, 1), 1, 254)
    scaled = (w * np.exp2(127.0 - byte)[:, None, :]).reshape(k, n).astype(np.float32)
    by_word = np.ascontiguousarray(scaled.reshape(k // 512, 128, 4, n).transpose(0, 1, 3, 2))
    if fmt == "e4m3":
        words = by_word.astype(ml_dtypes.float8_e4m3fn).view(np.uint8)
    else:
        c = by_word.astype(ml_dtypes.float4_e2m1fn).view(np.uint8) & 0xF
        words = (c[..., 0::2] | (c[..., 1::2] << 4)).reshape(k // 512, 128, 2 * n)
    return np.ascontiguousarray(words), np.ascontiguousarray(byte.astype(np.uint8).reshape(k // 512, 16, n))


def unpack_weight(words, scales, fmt):
    g, _, n = scales.shape
    words = np.ascontiguousarray(words).reshape(g, 128, n, -1)
    if fmt == "e4m3":
        vals = words.view(ml_dtypes.float8_e4m3fn).astype(np.float64)
    else:
        nib = np.empty((g, 128, n, 4), np.uint8)
        nib[..., 0::2] = words & 0xF
        nib[..., 1::2] = words >> 4
        vals = E2M1[nib]
    vals = vals * np.repeat(np.exp2(scales.astype(np.float64) - 127.0), 8, axis=1)[..., None]
    return vals.transpose(0, 1, 3, 2).reshape(g * 512, n)


K, T, E, C, N = 2048, 640, 10, 128, 256


def by_expert(wq, xq):
    return np.concatenate([wq[e].T @ xq[:, e * C:(e + 1) * C] for e in range(E)], axis=1)


def setup_inputs():
    n = np.random.standard_normal
    s = mx_kscale(K)[:, None]
    first = np.random.permutation(np.repeat(np.arange(E), T // E))
    second = (first + 1 + np.random.permutation(np.repeat(np.arange(E - 1), -(-T // (E - 1)))[:T])) % E
    while np.bincount(second, minlength=E).max() != T // E:
        load = np.bincount(second, minlength=E); hi, lo = int(load.argmax()), int(load.argmin())
        t = np.flatnonzero((second == hi) & (first != lo))[0]; second[t] = lo
    slot_token = np.empty(E * C, np.int64); pos = np.empty((2, T), np.int64); fill = np.zeros(E, np.int64)
    place = np.stack([np.random.permutation(C) for _ in range(E)])
    for r, deal in enumerate((first, second)):
        for t in np.random.permutation(T):
            e = deal[t]; j = e * C + place[e, fill[e]]; fill[e] += 1; slot_token[j] = t; pos[r, t] = j
    g = np.random.uniform(0.2, 0.8, T)
    x = pack_weight(n((K, T)) * s, "e4m3")
    return {
        "x_words": x[0],
        "x_scales": x[1],
        "w": (n((E + 1, K, N)) / np.sqrt(K) / s[None]).astype(np.float32),
        "gate": np.stack([np.tile(g, (N, 1)), np.tile(1.0 - g, (N, 1))]).astype(np.float32),
        "offs": striped(slot_token),
        "pos1": striped(pos[0]),
        "pos2": striped(pos[1]),
    }


def reference(x_words, x_scales, w, gate, offs, pos1, pos2):
    idx = unstriped(offs)
    wq = mxq(f64(w), 1, "e4m3")
    xs = unpack_weight(x_words, x_scales, "e4m3")
    ys = wq[E].T @ xs
    xq = unpack_weight(x_words, x_scales, "e4m3")[:, idx]
    y = by_expert(wq, xq)
    return ys + f64(gate[0]) * y[:, unstriped(pos1)] + f64(gate[1]) * y[:, unstriped(pos2)]

@@ -1,0 +1,158 @@
+from contextlib import ExitStack
+
+import concourse.mybir as mybir
+
+K, T, E, C, N = 2048, 640, 10, 128, 256
+FLOPS = 2 * K * N * (E * C + T)
+BYTES = (E + 1) * K * N * 4 + K * T + (K // 32) * T + 2 * T * 4 + 128 * (E * C + 2 * T) // 8 + N * T * 4
+
+F32 = mybir.dt.float32
+BF16 = mybir.dt.bfloat16
+I32 = mybir.dt.int32
+U32 = mybir.dt.uint32
+U16 = mybir.dt.uint16
+U8 = mybir.dt.uint8
+FP8X4 = mybir.dt.float8_e4m3fn_x4
+MULT = mybir.AluOpType.mult
+ADD = mybir.AluOpType.add
+
+P = 128
+PACK = 4
+K_PASS = P * PACK
+PASSES = K // K_PASS
+BLOCKS = N // P
+SLOTS = E * C
+GATHER = 2 * C
+BANK = 512
+
+
+def tile_moe_shr_lin_none_kernel(tc, x_words, x_scales, w, gate, offs, pos1, pos2, out):
+    nc = tc.nc
+    with ExitStack() as ctx:
+        keep = ctx.enter_context(tc.tile_pool(name="keep", bufs=1))
+        raws = ctx.enter_context(tc.tile_pool(name="raws", bufs=13))
+        stage = ctx.enter_context(tc.tile_pool(name="stage", bufs=8))
+        gathered = ctx.enter_context(tc.tile_pool(name="gathered", bufs=3))
+        psum = ctx.enter_context(tc.psum_pool(name="psum", bufs=2))
+        psum_shared = ctx.enter_context(tc.psum_pool(name="psum_shared", bufs=1))
+
+        slot_list = keep.tile([P, SLOTS // 16], U16, name="slot_list")
+        nc.sync.dma_start(slot_list[:], offs)
+        token_scales = keep.tile([P, T], U8, name="token_scales", align_bytes=64)
+        nc.vector.memset(token_scales[:].bitcast(I32), 0)
+        for q in range(4):
+            nc.sync.dma_start(token_scales[32 * q : 32 * q + 16, :].bitcast(I32), x_scales[:, 4 * q : 4 * q + 4, :].bitcast(I32))
+        token_words = keep.tile([P, PASSES, T], I32, name="token_words", align_bytes=64)
+        nc.sync.dma_start(token_words[:], x_words.rearrange("o p t r -> p o (t r)").bitcast(I32))
+        first_list = keep.tile([P, T // 16], U16, name="first_list")
+        nc.sync.dma_start(first_list[:], pos1)
+        second_list = keep.tile([P, T // 16], U16, name="second_list")
+        nc.sync.dma_start(second_list[:], pos2)
+
+        slot_sums = [keep.tile([P, SLOTS], F32, name=f"slot_sums{b}") for b in range(BLOCKS)]
+        gates = keep.tile([P, 2, T], F32, name="gates")
+
+        def gather_tokens(g):
+            entries = slot_list[:, g * GATHER // 16 : (g + 1) * GATHER // 16]
+            scales = gathered.tile([P, GATHER], U8, name="slot_scales", align_bytes=64)
+            nc.vector.tensor_copy(scales[:], token_scales[:].indirect(entries))
+            words = gathered.tile([P, PASSES, GATHER], U32, name="slot_words", align_bytes=64)
+            for o in range(PASSES):
+                nc.vector.tensor_copy(words[:, o, :], token_words[:, o, :].bitcast(U32).indirect(entries))
+            return words, scales
+
+        def interleave(copy, grouped, raw, o, lo, hi):
+            copy(
+                grouped[:, o, lo:hi, :].rearrange("p (c i) j -> p c j i", i=2),
+                raw[:, o, :, lo:hi].rearrange("p j (c i) -> p c j i", i=2),
+            )
+
+        def quantised_weights(e, passes, blocks, vector_columns, pool=stage, tag="grouped"):
+            count, width = len(passes), len(blocks) * P
+            raw = raws.tile([P, count, PACK, width], F32, name="raw")
+            rows = w[e, passes.start * K_PASS : passes.stop * K_PASS, blocks.start * P : blocks.stop * P]
+            if width == N:
+                nc.sync.dma_start(raw[:].rearrange("p o j n -> p o (j n)"), rows.rearrange("(o p j) n -> p o (j n)", p=P, j=PACK))
+            else:
+                for o in range(count):
+                    nc.sync.dma_start(raw[:, o, :, :], rows[o * K_PASS : (o + 1) * K_PASS, :].rearrange("(p j) n -> p j n", j=PACK))
+            grouped = pool.tile([P, count, width, PACK], BF16, name="grouped", tag=tag, align_bytes=64)
+            for o in range(count):
+                split = width - vector_columns if o == count - 1 else width
+                if split > 0:
+                    interleave(nc.scalar.copy, grouped, raw, o, 0, split)
+                if split < width:
+                    interleave(nc.vector.tensor_copy, grouped, raw, o, split, width)
+            codes = stage.tile([P, count * width], U32, name="codes", align_bytes=64)
+            scales = stage.tile([P, count * width], U8, name="scales", align_bytes=64)
+            nc.vector.quantize_mx(out=codes[:].bitcast(FP8X4), scales=scales[:], in_=grouped[:].rearrange("p o n j -> p (o n j)"))
+            return codes, scales
+
+        def multiply(acc, weights, passes, blocks, b, words, word_scales, columns):
+            codes, scales = weights
+            for o in passes:
+                lo = ((o - passes.start) * len(blocks) + b - blocks.start) * P
+                nc.tensor.matmul_mx(
+                    out=acc,
+                    lhsT=codes[:, lo : lo + P].bitcast(FP8X4),
+                    lhsT_scale=scales[:, lo : lo + P],
+                    rhs=words[:, o, columns].bitcast(FP8X4),
+                    rhs_scale=word_scales[4 * o : P, columns],
+                    start=(o == 0),
+                    stop=(o == PASSES - 1),
+                )
+
+        both = range(BLOCKS)
+        steady = [(range(0, 2), both, 0), (range(2, 4), both, N)]
+        last = [(range(0, 2), both, 0), (range(2, 3), both, N // 2), (range(3, 4), range(0, 1), 80), (range(3, 4), range(1, 2), 0)]
+        for experts in [range(0, 4), range(4, 8), range(8, 9), range(9, 10)]:
+            accs = [psum.tile([P, len(experts) * C], F32, name=f"acc{b}") for b in both]
+            for e in experts:
+                if e % 2 == 0:
+                    words, word_scales = gather_tokens(e // 2)
+                columns = slice((e % 2) * C, (e % 2 + 1) * C)
+                place = slice((e - experts.start) * C, (e - experts.start + 1) * C)
+                for passes, blocks, vector_columns in steady if e < E - 1 else last:
+                    weights = quantised_weights(e, passes, blocks, vector_columns)
+                    for b in blocks:
+                        multiply(accs[b][:, place], weights, passes, blocks, b, words, word_scales, columns)
+                        if e == experts.stop - 1 and passes.stop == PASSES:
+                            nc.scalar.copy(slot_sums[b][:, experts.start * C : experts.stop * C], accs[b][:])
+
+        nc.sync.dma_start(gates[:], gate[:, 0:P, :].rearrange("j p t -> p j t"))
+
+        def gated(b, choice, entries, tag):
+            part = keep.tile([P, T], F32, name="part", tag=tag, align_bytes=64)
+            nc.vector.tensor_tensor(part[:], slot_sums[b][:].indirect(entries[:]), gates[:, choice, :], MULT)
+            return part
+
+        first0 = gated(0, 0, first_list, "first0")
+        second0 = gated(0, 1, second_list, "second0")
+
+        spans = [slice(0, BANK), slice(BANK, T)]
+        shared = [[psum_shared.tile([P, s.stop - s.start], F32, name=f"shared{b}_{s.start}") for s in spans] for b in both]
+        for passes in [range(0, 2), range(2, 3), range(3, 4)]:
+            if passes.stop == PASSES:
+                weights = quantised_weights(E, passes, both, 0, keep, "first1")
+            else:
+                weights = quantised_weights(E, passes, both, 0)
+            for b in both:
+                for s, acc in zip(spans, shared[b]):
+                    multiply(acc[:], weights, passes, both, b, token_words, token_scales, s)
+
+        def with_shared(b, part, tag):
+            total = keep.tile([P, T], F32, name="total", tag=tag, align_bytes=64)
+            for s, acc in zip(spans, shared[b]):
+                nc.vector.tensor_tensor(total[:, s], part[:, s], acc[:], ADD)
+            return total
+
+        first1 = gated(1, 0, first_list, "first1")
+        routed0 = keep.tile([P, T], F32, name="routed0", tag="second1", align_bytes=64)
+        nc.vector.tensor_tensor(routed0[:], first0[:], second0[:], ADD)
+        result0 = with_shared(0, routed0, "result0")
+        nc.sync.dma_start(out[0:P, :], result0[:])
+        partial1 = with_shared(1, first1, "partial1")
+        second1 = gated(1, 1, second_list, "second1")
+        result1 = keep.tile([P, T], F32, name="result1")
+        nc.vector.tensor_tensor(result1[:], partial1[:], second1[:], ADD)
+        nc.sync.dma_start(out[P:N, :], result1[:])

@@ -1,6 +1,7 @@
 from contextlib import ExitStack
 
 import concourse.mybir as mybir
+from concourse.masks import make_identity
 
 K, T, E, C, N = 2048, 640, 10, 128, 256
 FLOPS = 2 * K * N * (E * C + T)
@@ -24,6 +25,8 @@ BLOCKS = N // P
 SLOTS = E * C
 GATHER = 2 * C
 BANK = 512
+SPLIT = 4
+TILES = T // P
 
 
 def tile_moe_shr_lin_none_kernel(tc, x_words, x_scales, w, gate, offs, pos1, pos2, out):
@@ -35,22 +38,40 @@ def tile_moe_shr_lin_none_kernel(tc, x_words, x_scales, w, gate, offs, pos1, pos
         gathered = ctx.enter_context(tc.tile_pool(name="gathered", bufs=3))
         psum = ctx.enter_context(tc.psum_pool(name="psum", bufs=2))
         psum_shared = ctx.enter_context(tc.psum_pool(name="psum_shared", bufs=1))
+        both = range(BLOCKS)
+        spans = [slice(0, BANK), slice(BANK, T)]
 
+        token_words = keep.tile([P, PASSES, T], I32, name="token_words", align_bytes=64)
+        nc.sync.dma_start(token_words[:], x_words.rearrange("o p t r -> p o (t r)").bitcast(I32))
         slot_list = keep.tile([P, SLOTS // 16], U16, name="slot_list")
         nc.sync.dma_start(slot_list[:], offs)
         token_scales = keep.tile([P, T], U8, name="token_scales", align_bytes=64)
         nc.vector.memset(token_scales[:].bitcast(I32), 0)
         for q in range(4):
             nc.sync.dma_start(token_scales[32 * q : 32 * q + 16, :].bitcast(I32), x_scales[:, 4 * q : 4 * q + 4, :].bitcast(I32))
-        token_words = keep.tile([P, PASSES, T], I32, name="token_words", align_bytes=64)
-        nc.sync.dma_start(token_words[:], x_words.rearrange("o p t r -> p o (t r)").bitcast(I32))
-        first_list = keep.tile([P, T // 16], U16, name="first_list")
-        nc.sync.dma_start(first_list[:], pos1)
-        second_list = keep.tile([P, T // 16], U16, name="second_list")
-        nc.sync.dma_start(second_list[:], pos2)
 
-        slot_sums = [keep.tile([P, SLOTS], F32, name=f"slot_sums{b}") for b in range(BLOCKS)]
+        slot_sums = [keep.tile([P, SLOTS], F32, name=f"slot_sums{b}") for b in both]
+        first_list = keep.tile([P, T // 16], U16, name="first_list")
+        second_list = keep.tile([P, T // 16], U16, name="second_list")
         gates = keep.tile([P, 2, T], F32, name="gates")
+
+        def spread_gates():
+            identity = keep.tile([P, P], F32, name="identity")
+            make_identity(nc, identity[:])
+            rows = keep.tile([P, P], F32, name="rows")
+            nc.vector.memset(rows[:], 0.0)
+            nc.sync.dma_start(rows[0 : 2 * TILES, :], gate[:, 0, :].rearrange("j (c t) -> j c t", t=P))
+            turned = psum_shared.tile([P, P], F32, name="turned", tag="shared0_512")
+            nc.tensor.transpose(turned[:], rows[:], identity[:])
+            columns = keep.tile([P, 2 * TILES], F32, name="columns")
+            nc.scalar.copy(columns[:], turned[:, 0 : 2 * TILES])
+            for choice in range(2):
+                for s in spans:
+                    spread = psum_shared.tile([P, s.stop - s.start], F32, name="spread", tag=f"shared{choice}_{s.start}")
+                    for c in range(s.start // P, s.stop // P):
+                        m = choice * TILES + c
+                        nc.tensor.transpose(spread[:, c * P - s.start : (c + 1) * P - s.start], columns[:, m : m + 1].to_broadcast([P, P]), identity[:])
+                    nc.scalar.copy(gates[:, choice, s], spread[:])
 
         def gather_tokens(g):
             entries = slot_list[:, g * GATHER // 16 : (g + 1) * GATHER // 16]
@@ -102,57 +123,63 @@ def tile_moe_shr_lin_none_kernel(tc, x_words, x_scales, w, gate, offs, pos1, pos
                     stop=(o == PASSES - 1),
                 )
 
-        both = range(BLOCKS)
-        steady = [(range(0, 2), both, 0), (range(2, 4), both, N)]
-        last = [(range(0, 2), both, 0), (range(2, 3), both, N // 2), (range(3, 4), range(0, 1), 80), (range(3, 4), range(1, 2), 0)]
-        for experts in [range(0, 4), range(4, 8), range(8, 9), range(9, 10)]:
-            accs = [psum.tile([P, len(experts) * C], F32, name=f"acc{b}") for b in both]
+        tokens = {}
+
+        def routed(experts, blocks, pieces, last_pieces, evacuate):
+            accs = {b: psum.tile([P, len(experts) * C], F32, name=f"acc{b}") for b in blocks}
             for e in experts:
-                if e % 2 == 0:
-                    words, word_scales = gather_tokens(e // 2)
+                if e // 2 not in tokens:
+                    tokens[e // 2] = gather_tokens(e // 2)
+                words, word_scales = tokens[e // 2]
                 columns = slice((e % 2) * C, (e % 2 + 1) * C)
                 place = slice((e - experts.start) * C, (e - experts.start + 1) * C)
-                for passes, blocks, vector_columns in steady if e < E - 1 else last:
+                for passes, vector_columns in pieces if e < experts.stop - 1 else last_pieces:
                     weights = quantised_weights(e, passes, blocks, vector_columns)
                     for b in blocks:
                         multiply(accs[b][:, place], weights, passes, blocks, b, words, word_scales, columns)
-                        if e == experts.stop - 1 and passes.stop == PASSES:
-                            nc.scalar.copy(slot_sums[b][:, experts.start * C : experts.stop * C], accs[b][:])
-
-        nc.sync.dma_start(gates[:], gate[:, 0:P, :].rearrange("j p t -> p j t"))
+            for b in blocks:
+                evacuate(slot_sums[b][:, experts.start * C : experts.stop * C], accs[b][:])
 
         def gated(b, choice, entries, tag):
             part = keep.tile([P, T], F32, name="part", tag=tag, align_bytes=64)
             nc.vector.tensor_tensor(part[:], slot_sums[b][:].indirect(entries[:]), gates[:, choice, :], MULT)
             return part
 
-        first0 = gated(0, 0, first_list, "first0")
-        second0 = gated(0, 1, second_list, "second0")
+        def added(first, second, name):
+            total = keep.tile([P, T], F32, name=name)
+            nc.vector.tensor_tensor(total[:], first[:], second[:], ADD)
+            return total
 
-        spans = [slice(0, BANK), slice(BANK, T)]
+        whole = [(range(0, 2), 0), (range(2, 4), N)]
+        spread_gates()
+        routed(range(0, 4), both, whole, whole, nc.scalar.copy)
+        nc.sync.dma_start(first_list[:], pos1)
+        nc.sync.dma_start(second_list[:], pos2)
+        routed(range(4, E - SPLIT), both, whole, whole, nc.scalar.copy)
+        fine = [(range(0, 2), 0), (range(2, 3), P // 2), (range(3, 4), 80)]
+        routed(range(E - SPLIT, E), range(0, 1), [(range(PASSES), P)], fine, nc.vector.tensor_copy)
+        combined0 = added(gated(0, 0, first_list, "first0"), gated(0, 1, second_list, "second0"), "combined0")
+        fine = [(range(0, 2), 0), (range(2, 3), 0), (range(3, 4), P // 2)]
+        routed(range(E - SPLIT, E), range(1, 2), [(range(PASSES), 0)], fine, nc.vector.tensor_copy)
+        first1 = gated(1, 0, first_list, "first1")
+
         shared = [[psum_shared.tile([P, s.stop - s.start], F32, name=f"shared{b}_{s.start}") for s in spans] for b in both]
-        for passes in [range(0, 2), range(2, 3), range(3, 4)]:
+        for o in range(PASSES):
+            passes = range(o, o + 1)
             if passes.stop == PASSES:
-                weights = quantised_weights(E, passes, both, 0, keep, "first1")
+                weights = quantised_weights(E, passes, both, 0, keep, "second1")
             else:
                 weights = quantised_weights(E, passes, both, 0)
             for b in both:
                 for s, acc in zip(spans, shared[b]):
                     multiply(acc[:], weights, passes, both, b, token_words, token_scales, s)
 
-        def with_shared(b, part, tag):
-            total = keep.tile([P, T], F32, name="total", tag=tag, align_bytes=64)
+        combined1 = added(first1, gated(1, 1, second_list, "second1"), "combined1")
+        for b, combined in zip(both, [combined0, combined1]):
+            result = keep.tile([P, T], F32, name=f"result{b}")
             for s, acc in zip(spans, shared[b]):
-                nc.vector.tensor_tensor(total[:, s], part[:, s], acc[:], ADD)
-            return total
-
-        first1 = gated(1, 0, first_list, "first1")
-        routed0 = keep.tile([P, T], F32, name="routed0", tag="second1", align_bytes=64)
-        nc.vector.tensor_tensor(routed0[:], first0[:], second0[:], ADD)
-        result0 = with_shared(0, routed0, "result0")
-        nc.sync.dma_start(out[0:P, :], result0[:])
-        partial1 = with_shared(1, first1, "partial1")
-        second1 = gated(1, 1, second_list, "second1")
-        result1 = keep.tile([P, T], F32, name="result1")
-        nc.vector.tensor_tensor(result1[:], partial1[:], second1[:], ADD)
-        nc.sync.dma_start(out[P:N, :], result1[:])
+                nc.vector.tensor_tensor(result[:, s], combined[:, s], acc[:], ADD)
+                if b == 1:
+                    nc.sync.dma_start(out[b * P : (b + 1) * P, s], result[:, s])
+            if b == 0:
+                nc.sync.dma_start(out[b * P : (b + 1) * P, :], result[:])

@@ -25,7 +25,6 @@ BLOCKS = N // P
 SLOTS = E * C
 GATHER = 2 * C
 BANK = 512
-SPLIT = 4
 TILES = T // P
 
 
@@ -82,11 +81,8 @@ def tile_moe_shr_lin_none_kernel(tc, x_words, x_scales, w, gate, offs, pos1, pos
                 nc.vector.tensor_copy(words[:, o, :], token_words[:, o, :].bitcast(U32).indirect(entries))
             return words, scales
 
-        def interleave(copy, grouped, raw, o, lo, hi):
-            copy(
-                grouped[:, o, lo:hi, :].rearrange("p (c i) j -> p c j i", i=2),
-                raw[:, o, :, lo:hi].rearrange("p j (c i) -> p c j i", i=2),
-            )
+        def interleave(copy, grouped, raw):
+            copy(grouped.rearrange("p o (c i) j -> p o c j i", i=2), raw.rearrange("p o j (c i) -> p o c j i", i=2))
 
         def quantised_weights(e, passes, blocks, vector_columns, pool=stage, tag="grouped"):
             count, width = len(passes), len(blocks) * P
@@ -98,12 +94,15 @@ def tile_moe_shr_lin_none_kernel(tc, x_words, x_scales, w, gate, offs, pos1, pos
                 for o in range(count):
                     nc.sync.dma_start(raw[:, o, :, :], rows[o * K_PASS : (o + 1) * K_PASS, :].rearrange("(p j) n -> p j n", j=PACK))
             grouped = pool.tile([P, count, width, PACK], BF16, name="grouped", tag=tag, align_bytes=64)
-            for o in range(count):
-                split = width - vector_columns if o == count - 1 else width
-                if split > 0:
-                    interleave(nc.scalar.copy, grouped, raw, o, 0, split)
-                if split < width:
-                    interleave(nc.vector.tensor_copy, grouped, raw, o, split, width)
+            if vector_columns == 0:
+                interleave(nc.scalar.copy, grouped[:], raw[:])
+            elif count == 2:
+                interleave(nc.scalar.copy, grouped[:, 0:1], raw[:, 0:1])
+                interleave(nc.vector.tensor_copy, grouped[:, 1:2], raw[:, 1:2])
+            else:
+                split = width - vector_columns
+                interleave(nc.scalar.copy, grouped[:, :, 0:split, :], raw[:, :, :, 0:split])
+                interleave(nc.vector.tensor_copy, grouped[:, :, split:width, :], raw[:, :, :, split:width])
             codes = stage.tile([P, count * width], U32, name="codes", align_bytes=64)
             scales = stage.tile([P, count * width], U8, name="scales", align_bytes=64)
             nc.vector.quantize_mx(out=codes[:].bitcast(FP8X4), scales=scales[:], in_=grouped[:].rearrange("p o n j -> p (o n j)"))
@@ -125,61 +124,75 @@ def tile_moe_shr_lin_none_kernel(tc, x_words, x_scales, w, gate, offs, pos1, pos
 
         tokens = {}
 
-        def routed(experts, blocks, pieces, last_pieces, evacuate):
-            accs = {b: psum.tile([P, len(experts) * C], F32, name=f"acc{b}") for b in blocks}
+        def routed(experts, evacuate):
+            accs = [psum.tile([P, len(experts) * C], F32, name=f"acc{b}") for b in both]
             for e in experts:
                 if e // 2 not in tokens:
                     tokens[e // 2] = gather_tokens(e // 2)
                 words, word_scales = tokens[e // 2]
                 columns = slice((e % 2) * C, (e % 2 + 1) * C)
                 place = slice((e - experts.start) * C, (e - experts.start + 1) * C)
-                for passes, vector_columns in pieces if e < experts.stop - 1 else last_pieces:
-                    weights = quantised_weights(e, passes, blocks, vector_columns)
+                for passes, blocks, vector_columns in pieces(e):
+                    if e == E - 1 and blocks.start == 1:
+                        weights = quantised_weights(e, passes, blocks, vector_columns, keep, "first0")
+                    else:
+                        weights = quantised_weights(e, passes, blocks, vector_columns)
                     for b in blocks:
                         multiply(accs[b][:, place], weights, passes, blocks, b, words, word_scales, columns)
-            for b in blocks:
-                evacuate(slot_sums[b][:, experts.start * C : experts.stop * C], accs[b][:])
+            for b in both:
+                evacuate[b](slot_sums[b][:, experts.start * C : experts.stop * C], accs[b][:])
 
-        def gated(b, choice, entries, tag):
-            part = keep.tile([P, T], F32, name="part", tag=tag, align_bytes=64)
-            nc.vector.tensor_tensor(part[:], slot_sums[b][:].indirect(entries[:]), gates[:, choice, :], MULT)
-            return part
+        def gated(part, b, choice, entries, s):
+            nc.vector.tensor_tensor(part[:, s], slot_sums[b][:].indirect(entries[:, s.start // 16 : s.stop // 16]), gates[:, choice, s], MULT)
 
-        def added(first, second, name):
-            total = keep.tile([P, T], F32, name=name)
-            nc.vector.tensor_tensor(total[:], first[:], second[:], ADD)
-            return total
+        def part_tile(tag):
+            return keep.tile([P, T], F32, name="part", tag=tag, align_bytes=64)
 
-        whole = [(range(0, 2), 0), (range(2, 4), N)]
+        def pieces(e):
+            if e == E - 1:
+                return [(range(0, 2), both, N), (range(2, 3), both, 160), (range(3, 4), range(0, 1), 80), (range(3, 4), range(1, 2), 0)]
+            return [(range(0, 2), both, N if e >= 5 else 0), (range(2, 4), both, N if e >= 2 else 0)]
+
         spread_gates()
-        routed(range(0, 4), both, whole, whole, nc.scalar.copy)
+        routed(range(0, 4), [nc.scalar.copy, nc.scalar.copy])
         nc.sync.dma_start(first_list[:], pos1)
         nc.sync.dma_start(second_list[:], pos2)
-        routed(range(4, E - SPLIT), both, whole, whole, nc.scalar.copy)
-        fine = [(range(0, 2), 0), (range(2, 3), P // 2), (range(3, 4), 80)]
-        routed(range(E - SPLIT, E), range(0, 1), [(range(PASSES), P)], fine, nc.vector.tensor_copy)
-        combined0 = added(gated(0, 0, first_list, "first0"), gated(0, 1, second_list, "second0"), "combined0")
-        fine = [(range(0, 2), 0), (range(2, 3), 0), (range(3, 4), P // 2)]
-        routed(range(E - SPLIT, E), range(1, 2), [(range(PASSES), 0)], fine, nc.vector.tensor_copy)
-        first1 = gated(1, 0, first_list, "first1")
+        routed(range(4, 7), [nc.scalar.copy, nc.scalar.copy])
+        routed(range(7, 10), [nc.vector.tensor_copy, nc.scalar.copy])
+
+        everyone = slice(0, T)
+        first0 = part_tile("first0")
+        gated(first0, 0, 0, first_list, everyone)
 
         shared = [[psum_shared.tile([P, s.stop - s.start], F32, name=f"shared{b}_{s.start}") for s in spans] for b in both]
         for o in range(PASSES):
             passes = range(o, o + 1)
-            if passes.stop == PASSES:
-                weights = quantised_weights(E, passes, both, 0, keep, "second1")
-            else:
-                weights = quantised_weights(E, passes, both, 0)
+            weights = quantised_weights(E, passes, both, 0, keep, f"shared_pass{o}")
             for b in both:
                 for s, acc in zip(spans, shared[b]):
                     multiply(acc[:], weights, passes, both, b, token_words, token_scales, s)
 
-        combined1 = added(first1, gated(1, 1, second_list, "second1"), "combined1")
-        for b, combined in zip(both, [combined0, combined1]):
-            result = keep.tile([P, T], F32, name=f"result{b}")
+        def with_shared(total, part, b):
             for s, acc in zip(spans, shared[b]):
-                nc.vector.tensor_tensor(result[:, s], combined[:, s], acc[:], ADD)
-                if b == 1:
-                    nc.sync.dma_start(out[b * P : (b + 1) * P, s], result[:, s])
-            if b == 0:
-                nc.sync.dma_start(out[b * P : (b + 1) * P, :], result[:])
+                nc.vector.tensor_tensor(total[:, s], part[:, s], acc[:], ADD)
+
+        second0 = part_tile("shared_pass0")
+        gated(second0, 0, 1, second_list, everyone)
+        first1 = part_tile("shared_pass2")
+        gated(first1, 1, 0, first_list, everyone)
+        halves = [slice(0, T // 2), slice(T // 2, T)]
+        second1 = [part_tile("shared_pass3"), None]
+        combined0 = part_tile("combined0")
+        nc.vector.tensor_tensor(combined0[:], first0[:], second0[:], ADD)
+        gated(second1[0], 1, 1, second_list, halves[0])
+        result0 = part_tile("result0")
+        with_shared(result0, combined0, 0)
+        nc.sync.dma_start(out[0:P, :], result0[:])
+        partial1 = part_tile("partial1")
+        with_shared(partial1, first1, 1)
+        second1[1] = part_tile("combined0")
+        gated(second1[1], 1, 1, second_list, halves[1])
+        result1 = part_tile("result1")
+        for s, second in zip(halves, second1):
+            nc.vector.tensor_tensor(result1[:, s], partial1[:, s], second[:, s], ADD)
+            nc.sync.dma_start(out[P:N, s], result1[:, s])

@@ -150,7 +150,7 @@ def tile_moe_shr_lin_none_kernel(tc, x_words, x_scales, w, gate, offs, pos1, pos
 
         def pieces(e):
             if e == E - 1:
-                return [(range(0, 2), both, N), (range(2, 3), both, 160), (range(3, 4), range(0, 1), 80), (range(3, 4), range(1, 2), 0)]
+                return [(range(0, 2), both, N), (range(2, 3), both, 160), (range(3, 4), range(0, 1), 80), (range(3, 4), range(1, 2), 80)]
             return [(range(0, 2), both, N if e >= 5 else 0), (range(2, 4), both, N if e >= 2 else 0)]
 
         spread_gates()
@@ -172,27 +172,23 @@ def tile_moe_shr_lin_none_kernel(tc, x_words, x_scales, w, gate, offs, pos1, pos
                 for s, acc in zip(spans, shared[b]):
                     multiply(acc[:], weights, passes, both, b, token_words, token_scales, s)
 
-        def with_shared(total, part, b):
-            for s, acc in zip(spans, shared[b]):
-                nc.vector.tensor_tensor(total[:, s], part[:, s], acc[:], ADD)
-
         second0 = part_tile("shared_pass0")
         gated(second0, 0, 1, second_list, everyone)
         first1 = part_tile("shared_pass2")
         gated(first1, 1, 0, first_list, everyone)
-        halves = [slice(0, T // 2), slice(T // 2, T)]
-        second1 = [part_tile("shared_pass3"), None]
+        second1 = part_tile("shared_pass3")
+        gated(second1, 1, 1, second_list, everyone)
         combined0 = part_tile("combined0")
         nc.vector.tensor_tensor(combined0[:], first0[:], second0[:], ADD)
-        gated(second1[0], 1, 1, second_list, halves[0])
         result0 = part_tile("result0")
-        with_shared(result0, combined0, 0)
+        for s, acc in zip(spans, shared[0]):
+            nc.vector.tensor_tensor(result0[:, s], combined0[:, s], acc[:], ADD)
         nc.sync.dma_start(out[0:P, :], result0[:])
-        partial1 = part_tile("partial1")
-        with_shared(partial1, first1, 1)
-        second1[1] = part_tile("combined0")
-        gated(second1[1], 1, 1, second_list, halves[1])
+        combined1 = part_tile("combined1")
+        nc.vector.tensor_tensor(combined1[:], first1[:], second1[:], ADD)
         result1 = part_tile("result1")
-        for s, second in zip(halves, second1):
-            nc.vector.tensor_tensor(result1[:, s], partial1[:, s], second[:, s], ADD)
+        for lo in range(0, T, BANK // 2):
+            s = slice(lo, min(lo + BANK // 2, T))
+            acc = shared[1][lo // BANK]
+            nc.vector.tensor_tensor(result1[:, s], combined1[:, s], acc[:, lo % BANK : lo % BANK + s.stop - s.start], ADD)
             nc.sync.dma_start(out[P:N, s], result1[:, s])

from contextlib import ExitStack

import concourse.mybir as mybir
from concourse.masks import make_identity

K, T, E, C, N = 2048, 640, 10, 128, 256
FLOPS = 2 * K * N * (E * C + T)
BYTES = (E + 1) * K * N * 4 + K * T + (K // 32) * T + 2 * T * 4 + 128 * (E * C + 2 * T) // 8 + N * T * 4

F32 = mybir.dt.float32
BF16 = mybir.dt.bfloat16
I32 = mybir.dt.int32
U32 = mybir.dt.uint32
U16 = mybir.dt.uint16
U8 = mybir.dt.uint8
FP8X4 = mybir.dt.float8_e4m3fn_x4
MULT = mybir.AluOpType.mult
ADD = mybir.AluOpType.add

P = 128
PACK = 4
K_PASS = P * PACK
PASSES = K // K_PASS
BLOCKS = N // P
SLOTS = E * C
GATHER = 2 * C
BANK = 512
TILES = T // P


def tile_moe_shr_lin_none_kernel(tc, x_words, x_scales, w, gate, offs, pos1, pos2, out):
    nc = tc.nc
    with ExitStack() as ctx:
        keep = ctx.enter_context(tc.tile_pool(name="keep", bufs=1))
        raws = ctx.enter_context(tc.tile_pool(name="raws", bufs=13))
        stage = ctx.enter_context(tc.tile_pool(name="stage", bufs=8))
        gathered = ctx.enter_context(tc.tile_pool(name="gathered", bufs=3))
        psum = ctx.enter_context(tc.psum_pool(name="psum", bufs=2))
        psum_shared = ctx.enter_context(tc.psum_pool(name="psum_shared", bufs=1))
        both = range(BLOCKS)
        spans = [slice(0, BANK), slice(BANK, T)]

        token_words = keep.tile([P, PASSES, T], I32, name="token_words", align_bytes=64)
        nc.sync.dma_start(token_words[:], x_words.rearrange("o p t r -> p o (t r)").bitcast(I32))
        slot_list = keep.tile([P, SLOTS // 16], U16, name="slot_list")
        nc.sync.dma_start(slot_list[:], offs)
        token_scales = keep.tile([P, T], U8, name="token_scales", align_bytes=64)
        nc.vector.memset(token_scales[:].bitcast(I32), 0)
        for q in range(4):
            nc.sync.dma_start(token_scales[32 * q : 32 * q + 16, :].bitcast(I32), x_scales[:, 4 * q : 4 * q + 4, :].bitcast(I32))

        slot_sums = [keep.tile([P, SLOTS], F32, name=f"slot_sums{b}") for b in both]
        first_list = keep.tile([P, T // 16], U16, name="first_list")
        second_list = keep.tile([P, T // 16], U16, name="second_list")
        gates = keep.tile([P, 2, T], F32, name="gates")

        def spread_gates():
            identity = keep.tile([P, P], F32, name="identity")
            make_identity(nc, identity[:])
            rows = keep.tile([P, P], F32, name="rows")
            nc.vector.memset(rows[:], 0.0)
            nc.sync.dma_start(rows[0 : 2 * TILES, :], gate[:, 0, :].rearrange("j (c t) -> j c t", t=P))
            turned = psum_shared.tile([P, P], F32, name="turned", tag="shared0_512")
            nc.tensor.transpose(turned[:], rows[:], identity[:])
            columns = keep.tile([P, 2 * TILES], F32, name="columns")
            nc.scalar.copy(columns[:], turned[:, 0 : 2 * TILES])
            for choice in range(2):
                for s in spans:
                    spread = psum_shared.tile([P, s.stop - s.start], F32, name="spread", tag=f"shared{choice}_{s.start}")
                    for c in range(s.start // P, s.stop // P):
                        m = choice * TILES + c
                        nc.tensor.transpose(spread[:, c * P - s.start : (c + 1) * P - s.start], columns[:, m : m + 1].to_broadcast([P, P]), identity[:])
                    nc.scalar.copy(gates[:, choice, s], spread[:])

        def gather_tokens(g):
            entries = slot_list[:, g * GATHER // 16 : (g + 1) * GATHER // 16]
            scales = gathered.tile([P, GATHER], U8, name="slot_scales", align_bytes=64)
            nc.vector.tensor_copy(scales[:], token_scales[:].indirect(entries))
            words = gathered.tile([P, PASSES, GATHER], U32, name="slot_words", align_bytes=64)
            for o in range(PASSES):
                nc.vector.tensor_copy(words[:, o, :], token_words[:, o, :].bitcast(U32).indirect(entries))
            return words, scales

        def interleave(copy, grouped, raw):
            copy(grouped.rearrange("p o (c i) j -> p o c j i", i=2), raw.rearrange("p o j (c i) -> p o c j i", i=2))

        def quantised_weights(e, passes, blocks, vector_columns, pool=stage, tag="grouped"):
            count, width = len(passes), len(blocks) * P
            raw = raws.tile([P, count, PACK, width], F32, name="raw")
            rows = w[e, passes.start * K_PASS : passes.stop * K_PASS, blocks.start * P : blocks.stop * P]
            if width == N:
                nc.sync.dma_start(raw[:].rearrange("p o j n -> p o (j n)"), rows.rearrange("(o p j) n -> p o (j n)", p=P, j=PACK))
            else:
                for o in range(count):
                    nc.sync.dma_start(raw[:, o, :, :], rows[o * K_PASS : (o + 1) * K_PASS, :].rearrange("(p j) n -> p j n", j=PACK))
            grouped = pool.tile([P, count, width, PACK], BF16, name="grouped", tag=tag, align_bytes=64)
            if vector_columns == 0:
                interleave(nc.scalar.copy, grouped[:], raw[:])
            elif count == 2:
                interleave(nc.scalar.copy, grouped[:, 0:1], raw[:, 0:1])
                interleave(nc.vector.tensor_copy, grouped[:, 1:2], raw[:, 1:2])
            else:
                split = width - vector_columns
                interleave(nc.scalar.copy, grouped[:, :, 0:split, :], raw[:, :, :, 0:split])
                interleave(nc.vector.tensor_copy, grouped[:, :, split:width, :], raw[:, :, :, split:width])
            codes = stage.tile([P, count * width], U32, name="codes", align_bytes=64)
            scales = stage.tile([P, count * width], U8, name="scales", align_bytes=64)
            nc.vector.quantize_mx(out=codes[:].bitcast(FP8X4), scales=scales[:], in_=grouped[:].rearrange("p o n j -> p (o n j)"))
            return codes, scales

        def multiply(acc, weights, passes, blocks, b, words, word_scales, columns):
            codes, scales = weights
            for o in passes:
                lo = ((o - passes.start) * len(blocks) + b - blocks.start) * P
                nc.tensor.matmul_mx(
                    out=acc,
                    lhsT=codes[:, lo : lo + P].bitcast(FP8X4),
                    lhsT_scale=scales[:, lo : lo + P],
                    rhs=words[:, o, columns].bitcast(FP8X4),
                    rhs_scale=word_scales[4 * o : P, columns],
                    start=(o == 0),
                    stop=(o == PASSES - 1),
                )

        tokens = {}

        def routed(experts, evacuate):
            accs = [psum.tile([P, len(experts) * C], F32, name=f"acc{b}") for b in both]
            for e in experts:
                if e // 2 not in tokens:
                    tokens[e // 2] = gather_tokens(e // 2)
                words, word_scales = tokens[e // 2]
                columns = slice((e % 2) * C, (e % 2 + 1) * C)
                place = slice((e - experts.start) * C, (e - experts.start + 1) * C)
                for passes, blocks, vector_columns in pieces(e):
                    if e == E - 1 and blocks.start == 1:
                        weights = quantised_weights(e, passes, blocks, vector_columns, keep, "first0")
                    else:
                        weights = quantised_weights(e, passes, blocks, vector_columns)
                    for b in blocks:
                        multiply(accs[b][:, place], weights, passes, blocks, b, words, word_scales, columns)
            for b in both:
                evacuate[b](slot_sums[b][:, experts.start * C : experts.stop * C], accs[b][:])

        def gated(part, b, choice, entries, s):
            nc.vector.tensor_tensor(part[:, s], slot_sums[b][:].indirect(entries[:, s.start // 16 : s.stop // 16]), gates[:, choice, s], MULT)

        def part_tile(tag):
            return keep.tile([P, T], F32, name="part", tag=tag, align_bytes=64)

        def pieces(e):
            if e == E - 1:
                return [(range(0, 2), both, N), (range(2, 3), both, 160), (range(3, 4), range(0, 1), 80), (range(3, 4), range(1, 2), 80)]
            return [(range(0, 2), both, N if e >= 5 else 0), (range(2, 4), both, N if e >= 2 else 0)]

        spread_gates()
        routed(range(0, 4), [nc.scalar.copy, nc.scalar.copy])
        nc.sync.dma_start(first_list[:], pos1)
        nc.sync.dma_start(second_list[:], pos2)
        routed(range(4, 7), [nc.scalar.copy, nc.scalar.copy])
        routed(range(7, 10), [nc.vector.tensor_copy, nc.scalar.copy])

        everyone = slice(0, T)
        first0 = part_tile("first0")
        gated(first0, 0, 0, first_list, everyone)

        shared = [[psum_shared.tile([P, s.stop - s.start], F32, name=f"shared{b}_{s.start}") for s in spans] for b in both]
        for o in range(PASSES):
            passes = range(o, o + 1)
            weights = quantised_weights(E, passes, both, 0, keep, f"shared_pass{o}")
            for b in both:
                for s, acc in zip(spans, shared[b]):
                    multiply(acc[:], weights, passes, both, b, token_words, token_scales, s)

        second0 = part_tile("shared_pass0")
        gated(second0, 0, 1, second_list, everyone)
        first1 = part_tile("shared_pass2")
        gated(first1, 1, 0, first_list, everyone)
        second1 = part_tile("shared_pass3")
        gated(second1, 1, 1, second_list, everyone)
        combined0 = part_tile("combined0")
        nc.vector.tensor_tensor(combined0[:], first0[:], second0[:], ADD)
        result0 = part_tile("result0")
        for s, acc in zip(spans, shared[0]):
            nc.vector.tensor_tensor(result0[:, s], combined0[:, s], acc[:], ADD)
        nc.sync.dma_start(out[0:P, :], result0[:])
        combined1 = part_tile("combined1")
        nc.vector.tensor_tensor(combined1[:], first1[:], second1[:], ADD)
        result1 = part_tile("result1")
        for lo in range(0, T, BANK // 2):
            s = slice(lo, min(lo + BANK // 2, T))
            acc = shared[1][lo // BANK]
            nc.vector.tensor_tensor(result1[:, s], combined1[:, s], acc[:, lo % BANK : lo % BANK + s.stop - s.start], ADD)
            nc.sync.dma_start(out[P:N, s], result1[:, s])
